import numpy as np, ml_dtypes
CORES = [37,45,53,61,69,109,117,125]
N = 8
NP, NBK, TK, CAP = 4, 8, 64, 10
DEST = [[6,4,6,7,6,7,6,4],[6,6,4,5,5,4,5,5],[5,4,4,6,7,5,7,7],[6,5,7,4,6,7,6,5]]
def setup_inputs(rng):
    return {"x": rng.standard_normal((N, 128, NBK * TK), dtype=np.float32).astype(ml_dtypes.bfloat16), "w": (rng.standard_normal((N, 128, 128), dtype=np.float32) / 8).astype(ml_dtypes.bfloat16)}
def setup_inputs_big(rng):
    d = setup_inputs(rng)
    for k in ("x", "w"): d[k] = (d[k].astype(np.float32) * 1024.0).astype(d[k].dtype)
    return d
def setup_inputs_small(rng):
    d = setup_inputs(rng)
    for k in ("x", "w"): d[k] = (d[k].astype(np.float32) * (1 / 1024.0)).astype(d[k].dtype)
    return d
def setup_inputs_apart(rng):
    d = setup_inputs(rng)
    f = (10.0 ** rng.permutation(np.linspace(-1.5, 1.5, N))).astype(np.float32).reshape(N, 1, 1)
    for k in ("x", "w"): d[k] = (d[k].astype(np.float32) * f).astype(d[k].dtype)
    return d
def reference(x, w):
    X, W = x.astype(np.float64), w.astype(np.float64)
    y = np.full((N, 128, CAP * TK), np.nan); n = [0] * N
    for p in range(NP):
        for c in range(NBK):
            q = DEST[p][c]
            y[q][:, TK * n[q]:TK * n[q] + TK] = W[q].T @ np.maximum(W[p].T @ X[p][:, TK * c:TK * c + TK], 0.0)
            n[q] += 1
    return {"y": y.astype(ml_dtypes.bfloat16 if x.dtype != np.float64 else np.float64)}

@@ -1,0 +1,151 @@
+from concourse.mybir import AluOpType
+
+NP, NBK, TK, CAP = 4, 8, 64, 10
+NPIECE = 4
+
+SCRATCH = {
+    "wsb": ("sbuf", [128, 128], "bfloat16"),
+    "xsb": ("sbuf", [128, NBK * TK], "bfloat16"),
+    "zero": ("sbuf", [128, NBK * TK], "float32"),
+    "hsb": ("sbuf", [128, NBK * TK], "bfloat16"),
+    "relay": ("sbuf", [128, NBK * TK], "bfloat16"),
+    "land": ("sbuf", [128, CAP * TK], "bfloat16"),
+    "ysb": ("sbuf", [128, CAP * TK], "bfloat16"),
+}
+for _i in range(NPIECE):
+    SCRATCH["ps%d" % _i] = ("psum", [128, 512], "float32")
+
+SEMAPHORES = (["ld", "zf", "sent", "rin", "st"] + ["mm%d" % i for i in range(NPIECE)]
+              + ["rl%d" % i for i in range(NPIECE)] + ["arr%d" % i for i in range(NP)])
+
+
+def _count(mask):
+    return len([b for b in range(16) if (mask >> b) & 1])
+
+
+def _plan(T, topo):
+    cores, dest = T.cores, T.tables["DEST"]
+    blocks, slot, owned = {}, {}, {}
+    for p in range(NP):
+        for c in range(NBK):
+            q = dest[p][c]
+            if (p, q) not in blocks:
+                blocks[(p, q)] = []
+                slot[(p, q)] = owned.get(q, 0)
+            blocks[(p, q)].append(c)
+            owned[q] = owned.get(q, 0) + 1
+    everyone = range(topo.CHIPS * topo.CORES_PER_CHIP)
+    sends, helpers, arrivals = {}, {}, {}
+    for p in range(NP):
+        pc = cores[p]
+        mine = [q for (pp, q) in blocks if pp == p]
+        mine.sort(key=lambda q: (topo.may_write(pc, cores[q]), -len(blocks[(p, q)]), -owned[q]))
+        near = [h for h in everyone if topo.chip(h) == topo.chip(pc) and h not in cores]
+        near.sort(key=lambda h: topo.die(h) == topo.die(pc))
+        sends[p], off = [], 0
+        for idx, q in enumerate(mine):
+            via = None
+            if not topo.may_write(pc, cores[q]):
+                via = [h for h in near if h not in helpers and topo.may_write(h, cores[q])][0]
+            piece = {"p": p, "q": q, "blocks": blocks[(p, q)], "n": len(blocks[(p, q)]), "hoff": off * TK,
+                     "yoff": slot[(p, q)] * TK, "via": via, "idx": idx}
+            if via is not None:
+                helpers[via] = piece
+            off += piece["n"]
+            sends[p].append(piece)
+            arrivals.setdefault(q, []).append(piece)
+    for q in arrivals:
+        arrivals[q].sort(key=lambda s: (s["via"] is not None, s["idx"], s["n"]))
+    return sends, arrivals, helpers
+
+
+def _near_mask(T, topo, s):
+    pc, far = T.cores[s["p"]], 0
+    for qc in T.cores[NP:]:
+        far |= topo.mask(pc, qc)
+    on = topo.mask(pc, s["via"])
+    return (on & ~far) or on
+
+
+def _far_mask(topo, src, dst):
+    return topo.mask(src, dst)
+
+
+def _write(g, T, topo, dst, out_ap, in_ap, remote_sem, mask):
+    rid, pid, _ = topo.addr(dst)
+    g.remote_dma(out_ap=out_ap, in_ap=in_ap, remote_sem=remote_sem, local_sem=T.sem.sent, pid=pid, routing_id=rid,
+                 dma_engine_mask=mask)
+    return _count(mask)
+
+
+def _sender(g, core, T, topo, pieces):
+    S = T.sem
+    g.scalar.dma_start(T.wsb[:], T.w[:]).then_inc(S.ld, 16)
+    g.sync.dma_start(T.xsb[:], T.x[:]).then_inc(S.ld, 16)
+    g.vector.memset(T.zero[:, 0:max(s["n"] for s in pieces) * TK], 0.0).then_inc(S.zf, 1)
+    g.tensor.wait_ge(S.ld, 32)
+    g.vector.wait_ge(S.zf, 1)
+    sent = 0
+    for i, s in enumerate(pieces):
+        ps, w = T["ps%d" % i], s["n"] * TK
+        runs = []
+        for c in s["blocks"]:
+            if runs and runs[-1][0] + runs[-1][1] == c:
+                runs[-1][1] += 1
+            else:
+                runs.append([c, 1])
+        j = 0
+        for c0, n in runs:
+            g.tensor.matmul(ps[:, j * TK:(j + n) * TK], T.wsb[:], T.xsb[:, c0 * TK:(c0 + n) * TK],
+                            start=True, stop=True).then_inc(S["mm%d" % i], 1)
+            j += n
+        g.vector.wait_ge(S["mm%d" % i], len(runs))
+        h = T.hsb[:, s["hoff"]:s["hoff"] + w]
+        g.vector.tensor_tensor(h, ps[:, 0:w], T.zero[:, 0:w], AluOpType.max).then_inc(S["rl%d" % i], 1)
+        g.wait_ge(S["rl%d" % i], 1)
+        if s["via"] is None:
+            dst = T.cores[s["q"]]
+            sent += _write(g, T, topo, dst, T.land[:, s["yoff"]:s["yoff"] + w], h, S["arr%d" % s["p"]],
+                           _far_mask(topo, core, dst))
+        else:
+            sent += _write(g, T, topo, s["via"], T.relay[:, 0:w], h, S.rin, _near_mask(T, topo, s))
+    g.wait_ge(S.sent, sent)
+
+
+def _helper(g, core, T, topo, s):
+    S, w = T.sem, s["n"] * TK
+    dst = T.cores[s["q"]]
+    g.wait_ge(S.rin, _count(_near_mask(T, topo, s)))
+    n = _write(g, T, topo, dst, T.land[:, s["yoff"]:s["yoff"] + w], T.relay[:, 0:w], S["arr%d" % s["p"]],
+               _far_mask(topo, core, dst))
+    g.wait_ge(S.sent, n)
+
+
+def _owner(g, core, T, topo, pieces):
+    S = T.sem
+    g.sync.dma_start(T.wsb[:], T.w[:]).then_inc(S.ld, 16)
+    g.tensor.wait_ge(S.ld, 16)
+    stores = [g.scalar, g.sync]
+    for i, s in enumerate(pieces):
+        ps, w, o = T["ps%d" % i], s["n"] * TK, s["yoff"]
+        last = s["via"] if s["via"] is not None else T.cores[s["p"]]
+        g.tensor.wait_ge(S["arr%d" % s["p"]], _count(_far_mask(topo, last, core)))
+        g.tensor.matmul(ps[:, 0:w], T.wsb[:], T.land[:, o:o + w], start=True, stop=True).then_inc(S["mm%d" % i], 1)
+        g.vector.wait_ge(S["mm%d" % i], 1)
+        g.vector.tensor_copy(T.ysb[:, o:o + w], ps[:, 0:w]).then_inc(S["rl%d" % i], 1)
+        qu = stores[i % 2]
+        qu.wait_ge(S["rl%d" % i], 1)
+        qu.dma_start(T.y[:, o:o + w], T.ysb[:, o:o + w]).then_inc(S.st, 16)
+    g.sync.wait_ge(S.st, 16 * len(pieces))
+
+
+def rank_program(g, core, T, topo):
+    sends, arrivals, helpers = _plan(T, topo)
+    rank = T.rank_of(core)
+    if rank is None:
+        if core in helpers:
+            _helper(g, core, T, topo, helpers[core])
+    elif rank < NP:
+        _sender(g, core, T, topo, sends[rank])
+    else:
+        _owner(g, core, T, topo, arrivals[rank])

@@ -15,7 +15,7 @@ SCRATCH = {
 for _i in range(NPIECE):
     SCRATCH["ps%d" % _i] = ("psum", [128, 512], "float32")
 
-SEMAPHORES = (["ld", "zf", "sent", "rin", "st"] + ["mm%d" % i for i in range(NPIECE)]
+SEMAPHORES = (["ld", "ld2", "zf", "sent", "rin", "st"] + ["mm%d" % i for i in range(NPIECE)]
               + ["rl%d" % i for i in range(NPIECE)] + ["arr%d" % i for i in range(NP)])
 
 
@@ -40,8 +40,13 @@ def _plan(T, topo):
         pc = cores[p]
         mine = [q for (pp, q) in blocks if pp == p]
         mine.sort(key=lambda q: (topo.may_write(pc, cores[q]), -len(blocks[(p, q)]), -owned[q]))
+        relayed = [q for q in mine if not topo.may_write(pc, cores[q])]
+        if relayed:
+            head = min(relayed, key=lambda q: blocks[(p, q)][-1] - blocks[(p, q)][0])
+            mine.remove(head)
+            mine.insert(0, head)
         near = [h for h in everyone if topo.chip(h) == topo.chip(pc) and h not in cores]
-        near.sort(key=lambda h: topo.die(h) == topo.die(pc))
+        near.sort(key=lambda h: topo.die(h) != topo.die(pc))
         sends[p], off = [], 0
         for idx, q in enumerate(mine):
             via = None
@@ -60,15 +65,10 @@ def _plan(T, topo):
 
 
 def _near_mask(T, topo, s):
-    pc, far = T.cores[s["p"]], 0
+    pc, on = T.cores[s["p"]], topo.mask(T.cores[s["p"]], s["via"])
     for qc in T.cores[NP:]:
-        far |= topo.mask(pc, qc)
-    on = topo.mask(pc, s["via"])
-    return (on & ~far) or on
-
-
-def _far_mask(topo, src, dst):
-    return topo.mask(src, dst)
+        on &= topo.mask(pc, qc)
+    return on
 
 
 def _write(g, T, topo, dst, out_ap, in_ap, remote_sem, mask):
@@ -80,13 +80,21 @@ def _write(g, T, topo, dst, out_ap, in_ap, remote_sem, mask):
 
 def _sender(g, core, T, topo, pieces):
     S = T.sem
+    lo, hi = pieces[0]["blocks"][0], pieces[0]["blocks"][-1] + 1
     g.scalar.dma_start(T.wsb[:], T.w[:]).then_inc(S.ld, 16)
-    g.sync.dma_start(T.xsb[:], T.x[:]).then_inc(S.ld, 16)
+    g.sync.dma_start(T.xsb[:, lo * TK:hi * TK], T.x[:, lo * TK:hi * TK]).then_inc(S.ld, 16)
+    rest = 0
+    for qu, a, b in ((g.scalar, 0, lo), (g.sync, hi, NBK)):
+        if b > a:
+            qu.dma_start(T.xsb[:, a * TK:b * TK], T.x[:, a * TK:b * TK]).then_inc(S.ld2, 16)
+            rest += 16
     g.vector.memset(T.zero[:, 0:max(s["n"] for s in pieces) * TK], 0.0).then_inc(S.zf, 1)
     g.tensor.wait_ge(S.ld, 32)
     g.vector.wait_ge(S.zf, 1)
     sent = 0
     for i, s in enumerate(pieces):
+        if i == 1 and rest:
+            g.tensor.wait_ge(S.ld2, rest)
         ps, w = T["ps%d" % i], s["n"] * TK
         runs = []
         for c in s["blocks"]:
@@ -106,7 +114,7 @@ def _sender(g, core, T, topo, pieces):
         if s["via"] is None:
             dst = T.cores[s["q"]]
             sent += _write(g, T, topo, dst, T.land[:, s["yoff"]:s["yoff"] + w], h, S["arr%d" % s["p"]],
-                           _far_mask(topo, core, dst))
+                           topo.mask(core, dst))
         else:
             sent += _write(g, T, topo, s["via"], T.relay[:, 0:w], h, S.rin, _near_mask(T, topo, s))
     g.wait_ge(S.sent, sent)
@@ -117,7 +125,7 @@ def _helper(g, core, T, topo, s):
     dst = T.cores[s["q"]]
     g.wait_ge(S.rin, _count(_near_mask(T, topo, s)))
     n = _write(g, T, topo, dst, T.land[:, s["yoff"]:s["yoff"] + w], T.relay[:, 0:w], S["arr%d" % s["p"]],
-               _far_mask(topo, core, dst))
+               topo.mask(core, dst))
     g.wait_ge(S.sent, n)
 
 
@@ -129,7 +137,7 @@ def _owner(g, core, T, topo, pieces):
     for i, s in enumerate(pieces):
         ps, w, o = T["ps%d" % i], s["n"] * TK, s["yoff"]
         last = s["via"] if s["via"] is not None else T.cores[s["p"]]
-        g.tensor.wait_ge(S["arr%d" % s["p"]], _count(_far_mask(topo, last, core)))
+        g.tensor.wait_ge(S["arr%d" % s["p"]], _count(topo.mask(last, core)))
         g.tensor.matmul(ps[:, 0:w], T.wsb[:], T.land[:, o:o + w], start=True, stop=True).then_inc(S["mm%d" % i], 1)
         g.vector.wait_ge(S["mm%d" % i], 1)
         g.vector.tensor_copy(T.ysb[:, o:o + w], ps[:, 0:w]).then_inc(S["rl%d" % i], 1)

from concourse.mybir import AluOpType

NP, NBK, TK, CAP = 4, 8, 64, 10
NPIECE = 4

SCRATCH = {
    "wsb": ("sbuf", [128, 128], "bfloat16"),
    "xsb": ("sbuf", [128, NBK * TK], "bfloat16"),
    "zero": ("sbuf", [128, NBK * TK], "float32"),
    "hsb": ("sbuf", [128, NBK * TK], "bfloat16"),
    "relay": ("sbuf", [128, NBK * TK], "bfloat16"),
    "land": ("sbuf", [128, CAP * TK], "bfloat16"),
    "ysb": ("sbuf", [128, CAP * TK], "bfloat16"),
}
for _i in range(NPIECE):
    SCRATCH["ps%d" % _i] = ("psum", [128, 512], "float32")

SEMAPHORES = (["ld", "ld2", "zf", "sent", "rin", "st"] + ["mm%d" % i for i in range(NPIECE)]
              + ["rl%d" % i for i in range(NPIECE)] + ["arr%d" % i for i in range(NP)])


def _count(mask):
    return len([b for b in range(16) if (mask >> b) & 1])


def _plan(T, topo):
    cores, dest = T.cores, T.tables["DEST"]
    blocks, slot, owned = {}, {}, {}
    for p in range(NP):
        for c in range(NBK):
            q = dest[p][c]
            if (p, q) not in blocks:
                blocks[(p, q)] = []
                slot[(p, q)] = owned.get(q, 0)
            blocks[(p, q)].append(c)
            owned[q] = owned.get(q, 0) + 1
    everyone = range(topo.CHIPS * topo.CORES_PER_CHIP)
    sends, helpers, arrivals = {}, {}, {}
    for p in range(NP):
        pc = cores[p]
        mine = [q for (pp, q) in blocks if pp == p]
        mine.sort(key=lambda q: (topo.may_write(pc, cores[q]), -len(blocks[(p, q)]), -owned[q]))
        relayed = [q for q in mine if not topo.may_write(pc, cores[q])]
        if relayed:
            head = min(relayed, key=lambda q: blocks[(p, q)][-1] - blocks[(p, q)][0])
            mine.remove(head)
            mine.insert(0, head)
        near = [h for h in everyone if topo.chip(h) == topo.chip(pc) and h not in cores]
        near.sort(key=lambda h: topo.die(h) != topo.die(pc))
        sends[p], off = [], 0
        for idx, q in enumerate(mine):
            via = None
            if not topo.may_write(pc, cores[q]):
                via = [h for h in near if h not in helpers and topo.may_write(h, cores[q])][0]
            piece = {"p": p, "q": q, "blocks": blocks[(p, q)], "n": len(blocks[(p, q)]), "hoff": off * TK,
                     "yoff": slot[(p, q)] * TK, "via": via, "idx": idx}
            if via is not None:
                helpers[via] = piece
            off += piece["n"]
            sends[p].append(piece)
            arrivals.setdefault(q, []).append(piece)
    for q in arrivals:
        arrivals[q].sort(key=lambda s: (s["via"] is not None, s["idx"], s["n"]))
    return sends, arrivals, helpers


def _near_mask(T, topo, s):
    pc, on = T.cores[s["p"]], topo.mask(T.cores[s["p"]], s["via"])
    for qc in T.cores[NP:]:
        on &= topo.mask(pc, qc)
    return on


def _write(g, T, topo, dst, out_ap, in_ap, remote_sem, mask):
    rid, pid, _ = topo.addr(dst)
    g.remote_dma(out_ap=out_ap, in_ap=in_ap, remote_sem=remote_sem, local_sem=T.sem.sent, pid=pid, routing_id=rid,
                 dma_engine_mask=mask)
    return _count(mask)


def _sender(g, core, T, topo, pieces):
    S = T.sem
    lo, hi = pieces[0]["blocks"][0], pieces[0]["blocks"][-1] + 1
    g.scalar.dma_start(T.wsb[:], T.w[:]).then_inc(S.ld, 16)
    g.sync.dma_start(T.xsb[:, lo * TK:hi * TK], T.x[:, lo * TK:hi * TK]).then_inc(S.ld, 16)
    rest = 0
    for qu, a, b in ((g.scalar, 0, lo), (g.sync, hi, NBK)):
        if b > a:
            qu.dma_start(T.xsb[:, a * TK:b * TK], T.x[:, a * TK:b * TK]).then_inc(S.ld2, 16)
            rest += 16
    g.vector.memset(T.zero[:, 0:max(s["n"] for s in pieces) * TK], 0.0).then_inc(S.zf, 1)
    g.tensor.wait_ge(S.ld, 32)
    g.vector.wait_ge(S.zf, 1)
    sent = 0
    for i, s in enumerate(pieces):
        if i == 1 and rest:
            g.tensor.wait_ge(S.ld2, rest)
        ps, w = T["ps%d" % i], s["n"] * TK
        runs = []
        for c in s["blocks"]:
            if runs and runs[-1][0] + runs[-1][1] == c:
                runs[-1][1] += 1
            else:
                runs.append([c, 1])
        j = 0
        for c0, n in runs:
            g.tensor.matmul(ps[:, j * TK:(j + n) * TK], T.wsb[:], T.xsb[:, c0 * TK:(c0 + n) * TK],
                            start=True, stop=True).then_inc(S["mm%d" % i], 1)
            j += n
        g.vector.wait_ge(S["mm%d" % i], len(runs))
        h = T.hsb[:, s["hoff"]:s["hoff"] + w]
        g.vector.tensor_tensor(h, ps[:, 0:w], T.zero[:, 0:w], AluOpType.max).then_inc(S["rl%d" % i], 1)
        g.wait_ge(S["rl%d" % i], 1)
        if s["via"] is None:
            dst = T.cores[s["q"]]
            sent += _write(g, T, topo, dst, T.land[:, s["yoff"]:s["yoff"] + w], h, S["arr%d" % s["p"]],
                           topo.mask(core, dst))
        else:
            sent += _write(g, T, topo, s["via"], T.relay[:, 0:w], h, S.rin, _near_mask(T, topo, s))
    g.wait_ge(S.sent, sent)


def _helper(g, core, T, topo, s):
    S, w = T.sem, s["n"] * TK
    dst = T.cores[s["q"]]
    g.wait_ge(S.rin, _count(_near_mask(T, topo, s)))
    n = _write(g, T, topo, dst, T.land[:, s["yoff"]:s["yoff"] + w], T.relay[:, 0:w], S["arr%d" % s["p"]],
               topo.mask(core, dst))
    g.wait_ge(S.sent, n)


def _owner(g, core, T, topo, pieces):
    S = T.sem
    g.sync.dma_start(T.wsb[:], T.w[:]).then_inc(S.ld, 16)
    g.tensor.wait_ge(S.ld, 16)
    stores = [g.scalar, g.sync]
    for i, s in enumerate(pieces):
        ps, w, o = T["ps%d" % i], s["n"] * TK, s["yoff"]
        last = s["via"] if s["via"] is not None else T.cores[s["p"]]
        g.tensor.wait_ge(S["arr%d" % s["p"]], _count(topo.mask(last, core)))
        g.tensor.matmul(ps[:, 0:w], T.wsb[:], T.land[:, o:o + w], start=True, stop=True).then_inc(S["mm%d" % i], 1)
        g.vector.wait_ge(S["mm%d" % i], 1)
        g.vector.tensor_copy(T.ysb[:, o:o + w], ps[:, 0:w]).then_inc(S["rl%d" % i], 1)
        qu = stores[i % 2]
        qu.wait_ge(S["rl%d" % i], 1)
        qu.dma_start(T.y[:, o:o + w], T.ysb[:, o:o + w]).then_inc(S.st, 16)
    g.sync.wait_ge(S.st, 16 * len(pieces))


def rank_program(g, core, T, topo):
    sends, arrivals, helpers = _plan(T, topo)
    rank = T.rank_of(core)
    if rank is None:
        if core in helpers:
            _helper(g, core, T, topo, helpers[core])
    elif rank < NP:
        _sender(g, core, T, topo, sends[rank])
    else:
        _owner(g, core, T, topo, arrivals[rank])
